import numpy as np
import ml_dtypes


def mxq(x, axis, fmt="e4m3"):
    dtype, down = {"e4m3": (ml_dtypes.float8_e4m3fn, 7), "e5m2": (ml_dtypes.float8_e5m2, 14)}[fmt]
    v = np.moveaxis(np.asarray(x, np.float32).astype(ml_dtypes.bfloat16).astype(np.float64), axis, -1)
    blocks = v.reshape(v.shape[:-1] + (-1, 32))
    amax = np.abs(blocks).max(-1, keepdims=True)
    byte = np.maximum(np.where(amax > 0, np.frexp(amax)[1] - 1 + 127, 0) - down, 1)
    scale = np.exp2(byte - 127.0)
    codes = (blocks / scale).astype(np.float32).astype(dtype).astype(np.float64)
    return np.moveaxis((codes * scale).reshape(v.shape), -1, axis)


WIDE = False


def mx_kscale(k):
    if not WIDE:
        return np.ones(k)
    levels = np.array([10, -10, 5, -5, 0])
    if k % 512:
        return np.exp2(np.random.permutation(np.resize(levels, k // 32))).repeat(32)
    a = np.empty((k // 512, 16))
    for p in range(k // 512):
        a[p, :8] = np.random.permutation(np.resize(levels, 8))
        for g in range(8):
            far = levels[np.abs(levels - a[p, g]) >= 10]
            a[p, g + 8] = far[np.random.randint(len(far))]
    return np.exp2(a.ravel()).repeat(32)


def f64(x):
    return np.asarray(x).astype(np.float64)


def striped(idx):
    return np.tile(idx.reshape(-1, 16).T, (8, 1)).astype(np.uint16)


def unstriped(offs):
    return offs[:16].T.reshape(-1).astype(np.int64)


E2M1 = np.array([0.0, 0.5, 1.0, 1.5, 2.0, 3.0, 4.0, 6.0, -0.0, -0.5, -1.0, -1.5, -2.0, -3.0, -4.0, -6.0])


def pack_weight(w, fmt):
    k, n = w.shape
    w = f64(np.asarray(w, np.float32).astype(ml_dtypes.bfloat16)).reshape(k // 32, 32, n)
    amax = np.abs(w).max(1)
    if fmt == "e4m3":
        byte = np.frexp(amax)[1] - 1 + 127 - 7
    else:
        mant, ex = np.frexp(amax / 6.0)
        byte = np.where(mant > 0.5, ex, ex - 1) + 127
    byte = np.clip(np.where(amax > 0, byte, 1), 1, 254)
    scaled = (w * np.exp2(127.0 - byte)[:, None, :]).reshape(k, n).astype(np.float32)
    by_word = np.ascontiguousarray(scaled.reshape(k // 512, 128, 4, n).transpose(0, 1, 3, 2))
    if fmt == "e4m3":
        words = by_word.astype(ml_dtypes.float8_e4m3fn).view(np.uint8)
    else:
        c = by_word.astype(ml_dtypes.float4_e2m1fn).view(np.uint8) & 0xF
        words = (c[..., 0::2] | (c[..., 1::2] << 4)).reshape(k // 512, 128, 2 * n)
    return np.ascontiguousarray(words), np.ascontiguousarray(byte.astype(np.uint8).reshape(k // 512, 16, n))


def unpack_weight(words, scales, fmt):
    g, _, n = scales.shape
    words = np.ascontiguousarray(words).reshape(g, 128, n, -1)
    if fmt == "e4m3":
        vals = words.view(ml_dtypes.float8_e4m3fn).astype(np.float64)
    else:
        nib = np.empty((g, 128, n, 4), np.uint8)
        nib[..., 0::2] = words & 0xF
        nib[..., 1::2] = words >> 4
        vals = E2M1[nib]
    vals = vals * np.repeat(np.exp2(scales.astype(np.float64) - 127.0), 8, axis=1)[..., None]
    return vals.transpose(0, 1, 3, 2).reshape(g * 512, n)


def gelu(v):
    return 0.5 * v * (1.0 + np.tanh(np.sqrt(2.0 / np.pi) * (v + 0.044715 * v**3)))


K, K2, T, S, H, T2, P, N = 1024, 512, 2048, 512, 1024, 2048, 1024, 512

def setup_inputs():
    n = np.random.standard_normal
    s = mx_kscale(K)[:, None]
    s2 = mx_kscale(K2)[:, None]
    u = mx_kscale(H)[:, None]
    d = {}
    d["tab_words"], d["tab_scales"] = pack_weight(n((K, T)) * s, "e4m3")
    d["tab2_words"], d["tab2_scales"] = pack_weight(n((K2, T)) * s2, "e4m3")
    d["offs"] = striped(np.random.permutation(T)[:S])
    d["offs2"] = striped(np.random.permutation(T)[:S])
    perm = np.random.permutation(T2)
    d["offs3"] = striped(perm[:S])
    d["offs4"] = striped(perm[S:2 * S])
    d["offs5"] = striped(np.random.permutation(T2)[:P])
    d["wa_words"], d["wa_scales"] = pack_weight(1.8 * n((K, H)) / K**0.5 / s, "e2m1")
    d["wb"] = (0.8 * n((K, H)) / K**0.5 / s * u.T).astype(np.float32)
    d["wq_words"], d["wq_scales"] = pack_weight(n((K2, H)) / K2**0.5 / s2 * np.sqrt(u).T, "e4m3")
    d["gain"] = (1.3 * np.exp(0.3 * n(H)) * u[:, 0]).astype(np.float32)
    d["page0"] = (n((H, T2)) * u).astype(np.float32)
    d["wg1"] = np.exp(0.3 * n((128, S))).astype(np.float32)
    d["wg2"] = np.exp(0.3 * n((128, S))).astype(np.float32)
    d["cap"] = ((0.7 + 0.5 * n(H)) * u[:, 0]).astype(np.float32)
    d["wo"] = (n((H, N)) / H**0.5 / u).astype(np.float32)
    return d

def reference(tab_words, tab_scales, tab2_words, tab2_scales, offs, offs2, offs3, offs4, offs5,
              wa_words, wa_scales, wb, wq_words, wq_scales, gain, page0, wg1, wg2, cap, wo):
    v = unpack_weight(tab_words, tab_scales, "e4m3")[:, unstriped(offs)]
    v2 = unpack_weight(tab2_words, tab2_scales, "e4m3")[:, unstriped(offs2)]
    a = unpack_weight(wa_words, wa_scales, "e2m1").T @ v
    b = mxq(f64(wb), 0, "e4m3").T @ v
    h1 = np.tanh(a) * f64(gain)[:, None] + b
    h2 = np.square(unpack_weight(wq_words, wq_scales, "e4m3").T @ v2)
    page = f64(page0).copy()
    page[:, unstriped(offs3)] = np.tile(f64(wg1), (H // 128, 1)) * h1
    page[:, unstriped(offs4)] = np.tile(f64(wg2), (H // 128, 1)) * h2
    x = np.minimum(page[:, unstriped(offs5)], f64(cap)[:, None])
    return mxq(f64(wo), 0, "e4m3").T @ mxq(x, 0, "e4m3")

@@ -1,0 +1,346 @@
+from contextlib import ExitStack
+
+import concourse.mybir as mybir
+from concourse.masks import make_identity
+
+F32 = mybir.dt.float32
+BF16 = mybir.dt.bfloat16
+I32 = mybir.dt.int32
+U32 = mybir.dt.uint32
+U16 = mybir.dt.uint16
+U8 = mybir.dt.uint8
+FP8X4 = mybir.dt.float8_e4m3fn_x4
+FP4X4 = mybir.dt.float4_e2m1fn_x4
+ACT = mybir.ActivationFunctionType
+ALU = mybir.AluOpType
+
+K, K2, T, S, H, T2, PICKS, N = 1024, 512, 2048, 512, 1024, 2048, 1024, 512
+FLOPS = 2 * K * H * S * 2 + 2 * K2 * H * S + 2 * H * N * PICKS
+
+P = 128
+PACK = 4
+PASS = P * PACK
+QUADS = 4
+ALIGN = 64
+
+
+def tile_list_tinnitus_session_ledger_kernel(
+    tc, tab_words, tab_scales, tab2_words, tab2_scales, offs, offs2, offs3, offs4, offs5,
+    wa_words, wa_scales, wb, wq_words, wq_scales, gain, page0, wg1, wg2, cap, wo, out,
+):
+    nc = tc.nc
+    halves = H // PASS
+    with ExitStack() as ctx:
+        keep = ctx.enter_context(tc.tile_pool(name="keep", bufs=1))
+        ring2 = ctx.enter_context(tc.tile_pool(name="ring2", bufs=2))
+        ring3 = ctx.enter_context(tc.tile_pool(name="ring3", bufs=3))
+        psum = ctx.enter_context(tc.psum_pool(name="psum", bufs=1))
+
+        def held(shape, dtype, name, tag=None):
+            return keep.tile(shape, dtype, name=name, tag=tag or name, align_bytes=ALIGN)
+
+        def bank(tag):
+            return psum.tile([P, PASS], F32, name=tag, tag=tag)
+
+        def load_list(src, name):
+            tile = keep.tile(list(src.shape), U16, name=name, tag=name)
+            nc.sync.dma_start(tile[:], src)
+            return tile
+
+        def zeroed_plane(shape, name):
+            tile = held(shape, U8, name)
+            nc.vector.memset(tile[:].bitcast(I32), 0)
+            return tile
+
+        def load_words(src, name, tag=None):
+            cols = src.shape[1]
+            tile = held([P, cols], I32, name, tag)
+            nc.sync.dma_start(tile[:], src.rearrange("p c i -> p (c i)").bitcast(I32))
+            return tile
+
+        page_rows = page0.rearrange("(b p t) c -> b t p c", b=halves, t=PACK)
+        pages = {}
+
+        def load_page(b, t):
+            pages[b, t] = held([P, T2], F32, f"page{b}{t}")
+            nc.sync.dma_start(pages[b, t][:], page_rows[b, t])
+
+        def load_wg(tile, src, t0, t1, queue=nc.sync):
+            rows = src.rearrange("(m t) j -> m t j", t=PACK)
+            for q in (0, 2, 1, 3):
+                queue.dma_start(tile[32 * q : 32 * q + 32, t0:t1, :], rows[:, t0:t1, :])
+
+        def gather_words(window, idx, name):
+            tile = held([P, S], U32, name)
+            nc.vector.tensor_copy(tile[:], window[:].bitcast(U32).indirect(idx[:]))
+            return tile
+
+        def gather_bytes(window, idx, name):
+            tile = held([P, S], U8, name)
+            nc.vector.tensor_copy(tile[:], window[:].indirect(idx[:]))
+            return tile
+
+        def mx(dst, lhs, lhs_scale, rhs, rhs_scale, start, stop, rhs_fmt=FP8X4):
+            nc.tensor.matmul_mx(dst, lhsT=lhs.bitcast(FP8X4), lhsT_scale=lhs_scale,
+                                rhs=rhs.bitcast(rhs_fmt), rhs_scale=rhs_scale, start=start, stop=stop)
+
+        tab2s = zeroed_plane([P, T], "tab2s")
+        wqs_raw = zeroed_plane([P, H], "wqs_raw")
+        tabs = zeroed_plane([P, T], "tabs")
+        was = zeroed_plane([P, 2, H], "was")
+        vs1 = zeroed_plane([P, S], "vs1")
+        ident = held([P, P], F32, "ident")
+        make_identity(nc, ident[:])
+
+        idx2 = load_list(offs2, "idx2")
+        for q in range(QUADS):
+            nc.sync.dma_start(tab2s[32 * q : 32 * q + 4, :].bitcast(I32), tab2_scales[0, 4 * q : 4 * q + 4, :].bitcast(I32))
+        tab2w = load_words(tab2_words[0], "tab2w")
+        wq_raw = load_words(wq_words[0], "wq_raw")
+        for q in range(QUADS):
+            nc.sync.dma_start(wqs_raw[32 * q : 32 * q + 4, :].bitcast(I32), wq_scales[0, 4 * q : 4 * q + 4, :].bitcast(I32))
+        load_page(0, 0)
+        idx4 = load_list(offs4, "idx4")
+        wg2t = held([P, PACK, S], F32, "wg2t")
+        load_wg(wg2t, wg2, 0, 1)
+        for q in range(QUADS):
+            nc.sync.dma_start(tabs[32 * q : 32 * q + 8, :].bitcast(I32), tab_scales[:, 4 * q : 4 * q + 4, :].bitcast(I32))
+        idx = load_list(offs, "idx")
+        load_page(1, 0)
+        tabw = [load_words(tab_words[0], "tabw0")]
+        vs0 = gather_bytes(tabs, idx, "vs0")
+        for q in range(QUADS):
+            nc.gpsimd.dma_start(vs1[32 * q : 32 * q + 4, :].bitcast(I32), vs0[32 * q + 4 : 32 * q + 8, :].bitcast(I32))
+        vs = [vs0, vs1]
+        load_wg(wg2t, wg2, 1, 2)
+        load_page(0, 1)
+        tabw.append(load_words(tab_words[1], "tabw1"))
+        load_page(1, 1)
+        load_wg(wg2t, wg2, 2, 4)
+
+        def load_rows(src):
+            raw = ring3.tile([P, PACK, PASS], F32, name="raw", tag="stage", align_bytes=ALIGN)
+            nc.sync.dma_start(raw[:], src.rearrange("(p j) c -> p j c", j=PACK))
+            return raw
+
+        def load_wb(a, b):
+            return load_rows(wb[a * PASS : (a + 1) * PASS, b * PASS : (b + 1) * PASS])
+
+        wb_raw = {}
+        wb_raw[0, 0] = load_wb(0, 0)
+        load_page(0, 2)
+        for q in range(QUADS):
+            nc.sync.dma_start(was[32 * q : 32 * q + 4, :, :].bitcast(I32),
+                              wa_scales[:, 4 * q : 4 * q + 4, :].rearrange("a r c -> r a c").bitcast(I32))
+        wa = held([P, 2, 2 * H], U8, "wa")
+        nc.sync.dma_start(wa[:].bitcast(I32), wa_words.rearrange("a p c -> p a c").bitcast(I32))
+        gain_t = held([P, halves, PACK], F32, "gain_t")
+        nc.sync.dma_start(gain_t[:], gain.rearrange("(b p t) -> p b t", b=halves, t=PACK))
+        load_page(1, 2)
+        wb_raw[1, 0] = load_wb(1, 0)
+        idx3 = load_list(offs3, "idx3")
+        wg1t = held([P, PACK, S], F32, "wg1t")
+        load_wg(wg1t, wg1, 0, 1)
+        load_page(0, 3)
+        load_page(1, 3)
+        load_wg(wg1t, wg1, 1, 4)
+        idx5 = load_list(offs5, "idx5")
+        cap_t = held([P, halves, PACK], F32, "cap_t")
+        nc.sync.dma_start(cap_t[:], cap.rearrange("(b p t) -> p b t", b=halves, t=PACK))
+        wb_raw[0, 1] = load_wb(0, 1)
+        wb_raw[1, 1] = load_wb(1, 1)
+        wo_raw = [load_rows(wo[b * PASS : (b + 1) * PASS, :]) for b in range(halves)]
+
+        v2s = gather_bytes(tab2s, idx2, "v2s")
+        wqs = held([P, H], U8, "wqs")
+        wq = held([P, H], I32, "wq")
+        for b in range(halves):
+            cols = slice(b * PASS, (b + 1) * PASS)
+            nc.vector.tensor_copy(wqs[:, cols].rearrange("p (t c i) -> p c t i", t=PACK, i=16),
+                                  wqs_raw[:, cols].rearrange("p (c i t) -> p c t i", t=PACK, i=16))
+        v2w = gather_words(tab2w, idx2, "v2w")
+        for b in range(halves):
+            cols = slice(b * PASS, (b + 1) * PASS)
+            nc.vector.tensor_copy(wq[:, cols].rearrange("p (t c i) -> p c t i", t=PACK, i=4),
+                                  wq_raw[:, cols].rearrange("p (c i t) -> p c t i", t=PACK, i=4))
+
+        h2 = [held([P, PACK, S], F32, f"h2_{b}", f"half{b}") for b in range(halves)]
+
+        def put_h2(b, t):
+            cols = slice(b * PASS + t * P, b * PASS + (t + 1) * P)
+            acc = bank(f"q{b}")
+            mx(acc[:], wq[:, cols], wqs[:, cols], v2w[:], v2s[:], True, True)
+            nc.scalar.activation(h2[b][:, t, :], acc[:], ACT.Square)
+            nc.vector.tensor_tensor(pages[b, t][:].indirect(idx4[:]), h2[b][:, t, :], wg2t[:, t, :], ALU.mult)
+
+        def round_rows(raw):
+            grouped = ring3.tile([P, PACK * PASS], BF16, name="grouped", tag="grouped", align_bytes=ALIGN)
+            nc.scalar.copy(grouped[:].rearrange("p (c i j) -> p c j i", i=4, j=PACK),
+                           raw[:].rearrange("p j (c i) -> p c j i", i=4))
+            return grouped
+
+        def quantise(grouped, name):
+            codes = held([P, PASS], U32, name)
+            scales = held([P, PASS], U8, name + "s")
+            nc.vector.quantize_mx(codes[:].bitcast(FP8X4), scales[:], grouped[:])
+            return codes, scales
+
+        put_h2(0, 0)
+        put_h2(1, 0)
+        vw = [gather_words(tabw[0], idx, "vw0")]
+        put_h2(0, 1)
+        vw.append(gather_words(tabw[1], idx, "vw1"))
+        put_h2(1, 1)
+        wbq = {}
+        wbq[0, 0] = quantise(round_rows(wb_raw[0, 0]), "wbq00")
+        put_h2(0, 2)
+        put_h2(1, 2)
+        wbq[1, 0] = quantise(round_rows(wb_raw[1, 0]), "wbq10")
+
+        chunks = S // P
+
+        def by_token(b, name, tag, func, operand):
+            res = held([P, chunks, PASS], F32, f"{name}{b}", tag)
+            for c in range(chunks):
+                tok = slice(c * P, (c + 1) * P)
+                acc = bank(f"a{c % 2}")
+                for a in range(2):
+                    codes, scales, fmt = operand(a)
+                    mx(acc[:], vw[a][:, tok], vs[a][:, tok], codes, scales, a == 0, a == 1, fmt)
+                nc.scalar.activation(res[:, c, :].rearrange("p (t m) -> p t m", t=PACK),
+                                     acc[:].rearrange("p (m t) -> p t m", t=PACK), func)
+            return res
+
+        def tanh_part(b):
+            return by_token(b, "tanh_t", "tanh_t", ACT.Tanh, lambda a: (
+                wa[:, a, 2 * b * PASS : 2 * (b + 1) * PASS], was[:, a, b * PASS : (b + 1) * PASS], FP4X4))
+
+        def linear_part(b):
+            return by_token(b, "lin_t", "tab2w", ACT.Copy, lambda a: (wbq[a, b][0][:], wbq[a, b][1][:], FP8X4))
+
+        def apply_gain(b, t, tanh_t):
+            cols = slice(t * P, (t + 1) * P)
+            turned = bank("x")
+            for c in range(chunks):
+                nc.tensor.transpose(turned[:, c * P : (c + 1) * P], tanh_t[:, c, cols], ident[:])
+            gained = ring2.tile([P, S], F32, name="gained", tag="gained")
+            nc.scalar.activation(gained[:], turned[:], ACT.Copy, scale=gain_t[:, b, t : t + 1])
+            back = bank("y")
+            for c in range(chunks):
+                nc.tensor.transpose(back[:, c * P : (c + 1) * P], gained[:, c * P : (c + 1) * P], ident[:])
+            gained_t = ring3.tile([P, S], F32, name="gained_t", tag="gained_t")
+            nc.scalar.copy(gained_t[:], back[:])
+            return gained_t
+
+        def make_h1(t, gained_t, lin_t, h1):
+            acc = bank(f"z{t % 2}")
+            for c in range(chunks):
+                dst = acc[:, c * P : (c + 1) * P]
+                nc.tensor.matmul(dst, gained_t[:, c * P : (c + 1) * P], ident[:], start=True, stop=False, is_transpose=True)
+                nc.tensor.matmul(dst, lin_t[:, c, t * P : (t + 1) * P], ident[:], start=False, stop=True, is_transpose=True)
+            nc.scalar.copy(h1[:, t, :], acc[:])
+
+        def put_h1(b, t, h1):
+            nc.vector.tensor_tensor(pages[b, t][:].indirect(idx3[:]), h1[:, t, :], wg1t[:, t, :], ALU.mult)
+
+        xq = [held([P, PICKS], U32, "xq0", "wq_raw"), held([P, PICKS], U32, "xq1", "wq")]
+        xs = [held([P, PICKS], U8, f"xs{b}") for b in range(halves)]
+
+        def fetch(b, j0, j1, tag):
+            xf = held([P, PACK, j1 - j0], F32, f"xf{b}_{j0}", tag)
+
+            def cap_at(t):
+                nc.vector.tensor_scalar(xf[:, t, :], xf[:, t, :], cap_t[:, b, t : t + 1], None, ALU.min)
+
+            for t in range(PACK):
+                nc.vector.tensor_copy(xf[:, t, :], pages[b, t][:].indirect(idx5[:, j0 // 16 : j1 // 16]))
+                if t > 0:
+                    cap_at(t - 1)
+            cap_at(PACK - 1)
+            return xf
+
+        def weave(xf, copy, tag=None):
+            width = xf.shape[2]
+            if tag:
+                grouped = held([P, PACK * width], BF16, "xgrouped", tag)
+            else:
+                grouped = ring3.tile([P, PACK * width], BF16, name="xgrouped", tag="grouped", align_bytes=ALIGN)
+            copy(grouped[:].rearrange("p (c i t) -> p c t i", i=4, t=PACK), xf.rearrange("p t (c i) -> p c t i", i=4))
+            return grouped
+
+        def quantise_x(b, j0, j1, grouped):
+            nc.vector.quantize_mx(xq[b][:, j0:j1].bitcast(FP8X4), xs[b][:, j0:j1], grouped[:])
+
+        tanh0 = tanh_part(0)
+        gained0 = [apply_gain(0, t, tanh0) for t in range(2)]
+        lin0 = linear_part(0)
+        put_h2(0, 3)
+        put_h2(1, 3)
+        h1a = held([P, PACK, S], F32, "h1a", "half0")
+        for t in range(PACK):
+            make_h1(t, gained0[t], lin0, h1a)
+            if t + 2 < PACK:
+                gained0.append(apply_gain(0, t + 2, tanh0))
+            put_h1(0, t, h1a)
+            if t < 2:
+                wbq[t, 1] = quantise(round_rows(wb_raw[t, 1]), f"wbq{t}1")
+        tanh1 = tanh_part(1)
+        lin1 = linear_part(1)
+        gained1 = [apply_gain(1, t, tanh1) for t in range(2)]
+        woq = [quantise(round_rows(wo_raw[b]), f"woq{b}") for b in range(halves)]
+        x0 = fetch(0, 0, PICKS, "half0")
+        h1b = held([P, PACK, S], F32, "h1b", "half1")
+        for t in range(PACK):
+            make_h1(t, gained1[t], lin1, h1b)
+            if t + 2 < PACK:
+                gained1.append(apply_gain(1, t + 2, tanh1))
+            put_h1(1, t, h1b)
+        quantise_x(0, 0, PICKS, weave(x0[:], nc.scalar.copy, "tab2w"))
+
+        out_rows = out.rearrange("(n p) j -> p n j", p=P)
+
+        def project_pass(dst, nt, b, j0, j1):
+            codes, scales = woq[b]
+            cols = slice(nt * P, (nt + 1) * P)
+            mx(dst, codes[:, cols], scales[:, cols], xq[b][:, j0:j1], xs[b][:, j0:j1], b == 0, b == 1)
+
+        first = [bank(tag) for tag in ("q0", "q1", "a0", "a1")]
+        for nt in range(4):
+            project_pass(first[nt][:], nt, 0, 0, 512)
+        x2 = fetch(1, 0, 512, "half1")
+        g2 = weave(x2[:], nc.scalar.copy, "wg2t")
+        x3 = fetch(1, 512, 768, "wg1t")
+        quantise_x(1, 0, 512, g2)
+        g3 = weave(x3[:], nc.scalar.copy)
+        quantise_x(1, 512, 768, g3)
+        x4 = fetch(1, 768, 1024, "wg2t")
+
+        staged = ring3.tile([P, PACK, 512], F32, name="staged0", tag="stage", align_bytes=ALIGN)
+        for nt in range(4):
+            project_pass(first[nt][:], nt, 1, 0, 512)
+            nc.scalar.copy(staged[:, nt, :], first[nt][:])
+            if nt % 2 == 1:
+                nc.sync.dma_start(out_rows[:, nt - 1 : nt + 1, 0:512], staged[:, nt - 1 : nt + 1, :])
+
+        staged = ring3.tile([P, PACK, 256], F32, name="staged1", tag="stage", align_bytes=ALIGN)
+        for pair, tag in enumerate(("z0", "z1")):
+            acc = bank(tag)
+            for e in range(2):
+                for b in range(halves):
+                    project_pass(acc[:, e * 256 : (e + 1) * 256], 2 * pair + e, b, 512, 768)
+            nc.scalar.copy(staged[:, 2 * pair : 2 * pair + 2, :], acc[:].rearrange("p (e j) -> p e j", e=2))
+        nc.sync.dma_start(out_rows[:, :, 512:768], staged[:])
+
+        last = [bank(tag) for tag in ("x", "y", "q0", "q1")]
+        for nt in range(4):
+            project_pass(last[nt][:, 0:256], nt, 0, 768, 1024)
+        g4 = weave(x4[:], nc.vector.tensor_copy)
+        quantise_x(1, 768, 1024, g4)
+        staged = ring3.tile([P, PACK, 256], F32, name="staged2", tag="stage", align_bytes=ALIGN)
+        for nt in range(4):
+            project_pass(last[nt][:, 0:256], nt, 1, 768, 1024)
+        for nt in (0, 2, 1, 3):
+            copy = nc.vector.tensor_copy if nt < 2 else nc.scalar.copy
+            copy(staged[:, nt, :], last[nt][:, 0:256])
+        for nt in (0, 2):
+            nc.scalar.dma_start(out_rows[:, nt : nt + 2, 768:1024], staged[:, nt : nt + 2, :])

@@ -22,6 +22,7 @@ PACK = 4
 PASS = P * PACK
 QUADS = 4
 ALIGN = 64
+VEC_ADDS = 2
 
 
 def tile_list_tinnitus_session_ledger_kernel(
@@ -92,10 +93,10 @@ def tile_list_tinnitus_session_ledger_kernel(
         ident = held([P, P], F32, "ident")
         make_identity(nc, ident[:])
 
+        tab2w = load_words(tab2_words[0], "tab2w")
         idx2 = load_list(offs2, "idx2")
         for q in range(QUADS):
             nc.sync.dma_start(tab2s[32 * q : 32 * q + 4, :].bitcast(I32), tab2_scales[0, 4 * q : 4 * q + 4, :].bitcast(I32))
-        tab2w = load_words(tab2_words[0], "tab2w")
         wq_raw = load_words(wq_words[0], "wq_raw")
         for q in range(QUADS):
             nc.sync.dma_start(wqs_raw[32 * q : 32 * q + 4, :].bitcast(I32), wq_scales[0, 4 * q : 4 * q + 4, :].bitcast(I32))
@@ -103,66 +104,65 @@ def tile_list_tinnitus_session_ledger_kernel(
         idx4 = load_list(offs4, "idx4")
         wg2t = held([P, PACK, S], F32, "wg2t")
         load_wg(wg2t, wg2, 0, 1)
-        for q in range(QUADS):
-            nc.sync.dma_start(tabs[32 * q : 32 * q + 8, :].bitcast(I32), tab_scales[:, 4 * q : 4 * q + 4, :].bitcast(I32))
-        idx = load_list(offs, "idx")
         load_page(1, 0)
-        tabw = [load_words(tab_words[0], "tabw0")]
-        vs0 = gather_bytes(tabs, idx, "vs0")
-        for q in range(QUADS):
-            nc.gpsimd.dma_start(vs1[32 * q : 32 * q + 4, :].bitcast(I32), vs0[32 * q + 4 : 32 * q + 8, :].bitcast(I32))
-        vs = [vs0, vs1]
-        load_wg(wg2t, wg2, 1, 2)
-        load_page(0, 1)
-        tabw.append(load_words(tab_words[1], "tabw1"))
-        load_page(1, 1)
-        load_wg(wg2t, wg2, 2, 4)
 
-        def load_rows(src):
-            raw = ring3.tile([P, PACK, PASS], F32, name="raw", tag="stage", align_bytes=ALIGN)
+        def load_rows(src, name, tag):
+            raw = held([P, PACK, PASS], F32, name, tag)
             nc.sync.dma_start(raw[:], src.rearrange("(p j) c -> p j c", j=PACK))
             return raw
 
-        def load_wb(a, b):
-            return load_rows(wb[a * PASS : (a + 1) * PASS, b * PASS : (b + 1) * PASS])
+        def load_wb(a, b, tag):
+            return load_rows(wb[a * PASS : (a + 1) * PASS, b * PASS : (b + 1) * PASS], f"wb{a}{b}", tag)
 
         wb_raw = {}
-        wb_raw[0, 0] = load_wb(0, 0)
-        load_page(0, 2)
+        for q in range(QUADS):
+            nc.sync.dma_start(tabs[32 * q : 32 * q + 8, :].bitcast(I32), tab_scales[:, 4 * q : 4 * q + 4, :].bitcast(I32))
+        idx = load_list(offs, "idx")
+        vs0 = gather_bytes(tabs, idx, "vs0")
+        vs = [vs0, vs1]
+        tabw = [load_words(tab_words[0], "tabw0")]
+        load_wg(wg2t, wg2, 1, 2)
+        load_page(0, 1)
+        tabw.append(load_words(tab_words[1], "tabw1"))
         for q in range(QUADS):
             nc.sync.dma_start(was[32 * q : 32 * q + 4, :, :].bitcast(I32),
                               wa_scales[:, 4 * q : 4 * q + 4, :].rearrange("a r c -> r a c").bitcast(I32))
-        wa = held([P, 2, 2 * H], U8, "wa")
-        nc.sync.dma_start(wa[:].bitcast(I32), wa_words.rearrange("a p c -> p a c").bitcast(I32))
         gain_t = held([P, halves, PACK], F32, "gain_t")
         nc.sync.dma_start(gain_t[:], gain.rearrange("(b p t) -> p b t", b=halves, t=PACK))
+        load_page(1, 1)
+        for q in range(QUADS):
+            nc.sync.dma_start(vs1[32 * q : 32 * q + 4, :].bitcast(I32), vs0[32 * q + 4 : 32 * q + 8, :].bitcast(I32))
+        wa = held([P, 2, 2 * H], U8, "wa")
+        nc.sync.dma_start(wa[:].bitcast(I32), wa_words.rearrange("a p c -> p a c").bitcast(I32))
+        load_wg(wg2t, wg2, 2, 3)
+        load_page(0, 2)
         load_page(1, 2)
-        wb_raw[1, 0] = load_wb(1, 0)
+        wb_raw[0, 0] = load_wb(0, 0, "stage0")
+        load_wg(wg2t, wg2, 3, 4)
+        load_page(0, 3)
+        wb_raw[1, 0] = load_wb(1, 0, "stage1")
+        load_page(1, 3)
         idx3 = load_list(offs3, "idx3")
         wg1t = held([P, PACK, S], F32, "wg1t")
-        load_wg(wg1t, wg1, 0, 1)
-        load_page(0, 3)
-        load_page(1, 3)
-        load_wg(wg1t, wg1, 1, 4)
+        load_wg(wg1t, wg1, 0, 2)
         idx5 = load_list(offs5, "idx5")
         cap_t = held([P, halves, PACK], F32, "cap_t")
         nc.sync.dma_start(cap_t[:], cap.rearrange("(b p t) -> p b t", b=halves, t=PACK))
-        wb_raw[0, 1] = load_wb(0, 1)
-        wb_raw[1, 1] = load_wb(1, 1)
-        wo_raw = [load_rows(wo[b * PASS : (b + 1) * PASS, :]) for b in range(halves)]
+        wb_raw[0, 1] = load_wb(0, 1, "stage2")
+        wb_raw[1, 1] = load_wb(1, 1, "stage0")
+        load_wg(wg1t, wg1, 2, 4)
+        wo_raw = [load_rows(wo[b * PASS : (b + 1) * PASS, :], f"wo{b}", f"stage{b + 1}") for b in range(halves)]
 
+        v2w = gather_words(tab2w, idx2, "v2w")
         v2s = gather_bytes(tab2s, idx2, "v2s")
         wqs = held([P, H], U8, "wqs")
         wq = held([P, H], I32, "wq")
         for b in range(halves):
             cols = slice(b * PASS, (b + 1) * PASS)
-            nc.vector.tensor_copy(wqs[:, cols].rearrange("p (t c i) -> p c t i", t=PACK, i=16),
-                                  wqs_raw[:, cols].rearrange("p (c i t) -> p c t i", t=PACK, i=16))
-        v2w = gather_words(tab2w, idx2, "v2w")
-        for b in range(halves):
-            cols = slice(b * PASS, (b + 1) * PASS)
             nc.vector.tensor_copy(wq[:, cols].rearrange("p (t c i) -> p c t i", t=PACK, i=4),
                                   wq_raw[:, cols].rearrange("p (c i t) -> p c t i", t=PACK, i=4))
+            nc.vector.tensor_copy(wqs[:, cols].rearrange("p (t c i) -> p c t i", t=PACK, i=16),
+                                  wqs_raw[:, cols].rearrange("p (c i t) -> p c t i", t=PACK, i=16))
 
         h2 = [held([P, PACK, S], F32, f"h2_{b}", f"half{b}") for b in range(halves)]
 
@@ -173,10 +173,14 @@ def tile_list_tinnitus_session_ledger_kernel(
             nc.scalar.activation(h2[b][:, t, :], acc[:], ACT.Square)
             nc.vector.tensor_tensor(pages[b, t][:].indirect(idx4[:]), h2[b][:, t, :], wg2t[:, t, :], ALU.mult)
 
-        def round_rows(raw):
+        def round_rows(raw, deal):
             grouped = ring3.tile([P, PACK * PASS], BF16, name="grouped", tag="grouped", align_bytes=ALIGN)
-            nc.scalar.copy(grouped[:].rearrange("p (c i j) -> p c j i", i=4, j=PACK),
-                           raw[:].rearrange("p j (c i) -> p c j i", i=4))
+            if deal:
+                nc.scalar.copy(grouped[:].rearrange("p (t m j) -> p m j t", t=PACK, j=PACK),
+                               raw[:].rearrange("p j (m t) -> p m j t", t=PACK))
+            else:
+                nc.scalar.copy(grouped[:].rearrange("p (c i j) -> p c j i", i=4, j=PACK),
+                               raw[:].rearrange("p j (c i) -> p c j i", i=4))
             return grouped
 
         def quantise(grouped, name):
@@ -185,60 +189,54 @@ def tile_list_tinnitus_session_ledger_kernel(
             nc.vector.quantize_mx(codes[:].bitcast(FP8X4), scales[:], grouped[:])
             return codes, scales
 
-        put_h2(0, 0)
-        put_h2(1, 0)
-        vw = [gather_words(tabw[0], idx, "vw0")]
-        put_h2(0, 1)
-        vw.append(gather_words(tabw[1], idx, "vw1"))
-        put_h2(1, 1)
-        wbq = {}
-        wbq[0, 0] = quantise(round_rows(wb_raw[0, 0]), "wbq00")
-        put_h2(0, 2)
-        put_h2(1, 2)
-        wbq[1, 0] = quantise(round_rows(wb_raw[1, 0]), "wbq10")
-
         chunks = S // P
 
-        def by_token(b, name, tag, func, operand):
-            res = held([P, chunks, PASS], F32, f"{name}{b}", tag)
+        def turn(dst, src, start=True, stop=True):
+            for c in range(chunks):
+                cols = slice(c * P, (c + 1) * P)
+                nc.tensor.matmul(dst[:, cols], src(c), ident[:], start=start and c == 0, stop=stop and c == chunks - 1, is_transpose=True)
+
+        def blocks(tile):
+            return lambda c: tile[:, c * P : (c + 1) * P]
+
+        def gained_tanh(b):
+            tanh_t = held([P, chunks, PASS], F32, f"tanh_t{b}", ("tanh_t", "stage0")[b])
             for c in range(chunks):
                 tok = slice(c * P, (c + 1) * P)
                 acc = bank(f"a{c % 2}")
                 for a in range(2):
-                    codes, scales, fmt = operand(a)
-                    mx(acc[:], vw[a][:, tok], vs[a][:, tok], codes, scales, a == 0, a == 1, fmt)
-                nc.scalar.activation(res[:, c, :].rearrange("p (t m) -> p t m", t=PACK),
-                                     acc[:].rearrange("p (m t) -> p t m", t=PACK), func)
-            return res
+                    mx(acc[:], vw[a][:, tok], vs[a][:, tok], wa[:, a, 2 * b * PASS : 2 * (b + 1) * PASS],
+                       was[:, a, b * PASS : (b + 1) * PASS], a == 0, a == 1, FP4X4)
+                nc.scalar.activation(tanh_t[:, c, :].rearrange("p (t m) -> p t m", t=PACK),
+                                     acc[:].rearrange("p (m t) -> p t m", t=PACK), ACT.Tanh)
+            gained = held([P, PACK, S], F32, f"gained{b}", ("tab2w", "tabw0")[b])
+            for t in range(PACK):
+                turned = bank(("x", "y")[t % 2])
+                turn(turned, lambda c: tanh_t[:, c, t * P : (t + 1) * P])
+                nc.scalar.activation(gained[:, t, :], turned[:], ACT.Copy, scale=gain_t[:, b, t : t + 1])
+            return gained
 
-        def tanh_part(b):
-            return by_token(b, "tanh_t", "tanh_t", ACT.Tanh, lambda a: (
-                wa[:, a, 2 * b * PASS : 2 * (b + 1) * PASS], was[:, a, b * PASS : (b + 1) * PASS], FP4X4))
+        def linear(b, t, tag):
+            acc = bank(tag)
+            for a in range(2):
+                codes, scales = wbq[a, b]
+                mx(acc[:], codes[:, t * P : (t + 1) * P], scales[:, t * P : (t + 1) * P], vw[a][:], vs[a][:], a == 0, a == 1)
+            return acc
 
-        def linear_part(b):
-            return by_token(b, "lin_t", "tab2w", ACT.Copy, lambda a: (wbq[a, b][0][:], wbq[a, b][1][:], FP8X4))
+        def add_on_vector(b, t, gained, h1):
+            nc.vector.tensor_tensor(h1[:, t, :], linear(b, t, ("q0", "q1", "w0", "w1")[t])[:], gained[:, t, :], ALU.add)
 
-        def apply_gain(b, t, tanh_t):
-            cols = slice(t * P, (t + 1) * P)
-            turned = bank("x")
-            for c in range(chunks):
-                nc.tensor.transpose(turned[:, c * P : (c + 1) * P], tanh_t[:, c, cols], ident[:])
-            gained = ring2.tile([P, S], F32, name="gained", tag="gained")
-            nc.scalar.activation(gained[:], turned[:], ACT.Copy, scale=gain_t[:, b, t : t + 1])
-            back = bank("y")
-            for c in range(chunks):
-                nc.tensor.transpose(back[:, c * P : (c + 1) * P], gained[:, c * P : (c + 1) * P], ident[:])
-            gained_t = ring3.tile([P, S], F32, name="gained_t", tag="gained_t")
-            nc.scalar.copy(gained_t[:], back[:])
-            return gained_t
-
-        def make_h1(t, gained_t, lin_t, h1):
-            acc = bank(f"z{t % 2}")
-            for c in range(chunks):
-                dst = acc[:, c * P : (c + 1) * P]
-                nc.tensor.matmul(dst, gained_t[:, c * P : (c + 1) * P], ident[:], start=True, stop=False, is_transpose=True)
-                nc.tensor.matmul(dst, lin_t[:, c, t * P : (t + 1) * P], ident[:], start=False, stop=True, is_transpose=True)
-            nc.scalar.copy(h1[:, t, :], acc[:])
+        def add_on_tensor(b, t, gained, h1):
+            lin = ring2.tile([P, S], F32, name="lin", tag="lin")
+            nc.scalar.copy(lin[:], linear(b, t, f"{'aq'[b]}{t % 2}")[:])
+            total = bank(f"w{t % 2}")
+            turn(total, blocks(gained[:, t, :]), stop=False)
+            turn(total, blocks(lin), start=False)
+            total_t = ring2.tile([P, S], F32, name="total_t", tag="total_t")
+            nc.scalar.copy(total_t[:], total[:])
+            back = bank(("x", "y")[t % 2])
+            turn(back, blocks(total_t))
+            nc.scalar.copy(h1[:, t, :], back[:])
 
         def put_h1(b, t, h1):
             nc.vector.tensor_tensor(pages[b, t][:].indirect(idx3[:]), h1[:, t, :], wg1t[:, t, :], ALU.mult)
@@ -271,42 +269,59 @@ def tile_list_tinnitus_session_ledger_kernel(
         def quantise_x(b, j0, j1, grouped):
             nc.vector.quantize_mx(xq[b][:, j0:j1].bitcast(FP8X4), xs[b][:, j0:j1], grouped[:])
 
-        tanh0 = tanh_part(0)
-        gained0 = [apply_gain(0, t, tanh0) for t in range(2)]
-        lin0 = linear_part(0)
-        put_h2(0, 3)
-        put_h2(1, 3)
-        h1a = held([P, PACK, S], F32, "h1a", "half0")
+        wbq = {}
+        put_h2(0, 0)
+        put_h2(1, 0)
+        vw = [gather_words(tabw[a], idx, f"vw{a}") for a in range(2)]
+        for a in range(2):
+            wbq[a, 0] = quantise(round_rows(wb_raw[a, 0], True), f"wbq{a}0")
+        for t in range(1, PACK):
+            put_h2(0, t)
+            put_h2(1, t)
+        gained0 = gained_tanh(0)
+        h1a = held([P, PACK, S], F32, "h1a", "h1a")
         for t in range(PACK):
-            make_h1(t, gained0[t], lin0, h1a)
-            if t + 2 < PACK:
-                gained0.append(apply_gain(0, t + 2, tanh0))
+            if t < VEC_ADDS:
+                add_on_vector(0, t, gained0, h1a)
+            else:
+                add_on_tensor(0, t, gained0, h1a)
+        for t in range(PACK):
             put_h1(0, t, h1a)
-            if t < 2:
-                wbq[t, 1] = quantise(round_rows(wb_raw[t, 1]), f"wbq{t}1")
-        tanh1 = tanh_part(1)
-        lin1 = linear_part(1)
-        gained1 = [apply_gain(1, t, tanh1) for t in range(2)]
-        woq = [quantise(round_rows(wo_raw[b]), f"woq{b}") for b in range(halves)]
-        x0 = fetch(0, 0, PICKS, "half0")
+        for a in range(2):
+            wbq[a, 1] = quantise(round_rows(wb_raw[a, 1], True), f"wbq{a}1")
+        gained1 = gained_tanh(1)
+        x0 = fetch(0, 0, PICKS, "h1a")
         h1b = held([P, PACK, S], F32, "h1b", "half1")
         for t in range(PACK):
-            make_h1(t, gained1[t], lin1, h1b)
-            if t + 2 < PACK:
-                gained1.append(apply_gain(1, t + 2, tanh1))
+            add_on_tensor(1, t, gained1, h1b)
+        for t in range(PACK):
             put_h1(1, t, h1b)
-        quantise_x(0, 0, PICKS, weave(x0[:], nc.scalar.copy, "tab2w"))
+        woq = [quantise(round_rows(wo_raw[b], False), f"woq{b}") for b in range(halves)]
+        g0 = held([P, PACK * PICKS], BF16, "g0", "stage0")
+        for j0 in (0, 512):
+            part = g0[:, PACK * j0 : PACK * (j0 + 512)]
+            nc.scalar.copy(part.rearrange("p (c i t) -> p c t i", i=4, t=PACK), x0[:, :, j0 : j0 + 512].rearrange("p t (c i) -> p c t i", i=4))
+            nc.vector.quantize_mx(xq[0][:, j0 : j0 + 512].bitcast(FP8X4), xs[0][:, j0 : j0 + 512], part)
 
         out_rows = out.rearrange("(n p) j -> p n j", p=P)
 
-        def project_pass(dst, nt, b, j0, j1):
+        def project_pass(dst, nt, b, j0, j1, start, stop):
             codes, scales = woq[b]
             cols = slice(nt * P, (nt + 1) * P)
-            mx(dst, codes[:, cols], scales[:, cols], xq[b][:, j0:j1], xs[b][:, j0:j1], b == 0, b == 1)
+            mx(dst, codes[:, cols], scales[:, cols], xq[b][:, j0:j1], xs[b][:, j0:j1], start, stop)
+
+        def project_narrow(banks, b, j0):
+            for nt in range(4):
+                e = nt % 2
+                project_pass(banks[nt // 2][:, e * 256 : (e + 1) * 256], nt, b, j0, j0 + 256, b == 0 and e == 0, b == 1 and e == 1)
 
         first = [bank(tag) for tag in ("q0", "q1", "a0", "a1")]
+        second = [bank(tag) for tag in ("w0", "w1")]
+        third = [bank(tag) for tag in ("x", "y")]
         for nt in range(4):
-            project_pass(first[nt][:], nt, 0, 0, 512)
+            project_pass(first[nt][:], nt, 0, 0, 512, True, False)
+        project_narrow(second, 0, 512)
+        project_narrow(third, 0, 768)
         x2 = fetch(1, 0, 512, "half1")
         g2 = weave(x2[:], nc.scalar.copy, "wg2t")
         x3 = fetch(1, 512, 768, "wg1t")
@@ -315,32 +330,22 @@ def tile_list_tinnitus_session_ledger_kernel(
         quantise_x(1, 512, 768, g3)
         x4 = fetch(1, 768, 1024, "wg2t")
 
-        staged = ring3.tile([P, PACK, 512], F32, name="staged0", tag="stage", align_bytes=ALIGN)
+        staged = held([P, PACK, 512], F32, "staged0", "stage1")
         for nt in range(4):
-            project_pass(first[nt][:], nt, 1, 0, 512)
+            project_pass(first[nt][:], nt, 1, 0, 512, False, True)
             nc.scalar.copy(staged[:, nt, :], first[nt][:])
             if nt % 2 == 1:
                 nc.sync.dma_start(out_rows[:, nt - 1 : nt + 1, 0:512], staged[:, nt - 1 : nt + 1, :])
 
-        staged = ring3.tile([P, PACK, 256], F32, name="staged1", tag="stage", align_bytes=ALIGN)
-        for pair, tag in enumerate(("z0", "z1")):
-            acc = bank(tag)
-            for e in range(2):
-                for b in range(halves):
-                    project_pass(acc[:, e * 256 : (e + 1) * 256], 2 * pair + e, b, 512, 768)
-            nc.scalar.copy(staged[:, 2 * pair : 2 * pair + 2, :], acc[:].rearrange("p (e j) -> p e j", e=2))
+        staged = held([P, PACK, 256], F32, "staged1", "stage2")
+        project_narrow(second, 1, 512)
+        for pair in range(2):
+            nc.scalar.copy(staged[:, 2 * pair : 2 * pair + 2, :], second[pair][:].rearrange("p (e j) -> p e j", e=2))
         nc.sync.dma_start(out_rows[:, :, 512:768], staged[:])
 
-        last = [bank(tag) for tag in ("x", "y", "q0", "q1")]
-        for nt in range(4):
-            project_pass(last[nt][:, 0:256], nt, 0, 768, 1024)
-        g4 = weave(x4[:], nc.vector.tensor_copy)
-        quantise_x(1, 768, 1024, g4)
-        staged = ring3.tile([P, PACK, 256], F32, name="staged2", tag="stage", align_bytes=ALIGN)
-        for nt in range(4):
-            project_pass(last[nt][:, 0:256], nt, 1, 768, 1024)
-        for nt in (0, 2, 1, 3):
-            copy = nc.vector.tensor_copy if nt < 2 else nc.scalar.copy
-            copy(staged[:, nt, :], last[nt][:, 0:256])
-        for nt in (0, 2):
-            nc.scalar.dma_start(out_rows[:, nt : nt + 2, 768:1024], staged[:, nt : nt + 2, :])
+        quantise_x(1, 768, 1024, weave(x4[:], nc.vector.tensor_copy))
+        staged = held([P, PACK, 256], F32, "staged2", "tanh_t")
+        project_narrow(third, 1, 768)
+        for pair, (copy, queue) in enumerate(((nc.vector.tensor_copy, nc.sync), (nc.scalar.copy, nc.scalar))):
+            copy(staged[:, 2 * pair : 2 * pair + 2, :], third[pair][:].rearrange("p (e j) -> p e j", e=2))
+            queue.dma_start(out_rows[:, 2 * pair : 2 * pair + 2, 768:1024], staged[:, 2 * pair : 2 * pair + 2, :])

@@ -66,10 +66,15 @@ def tile_list_tinnitus_session_ledger_kernel(
             pages[b, t] = held([P, T2], F32, f"page{b}{t}")
             nc.sync.dma_start(pages[b, t][:], page_rows[b, t])
 
-        def load_wg(tile, src, t0, t1, queue=nc.sync):
+        def load_wg(src, name):
+            tile = ring2.tile([P, S], F32, name=name, tag="lin")
+            nc.sync.dma_start(tile[:], src)
+            return tile
+
+        def load_dealt(tile, src, t0, t1):
             rows = src.rearrange("(m t) j -> m t j", t=PACK)
             for q in (0, 2, 1, 3):
-                queue.dma_start(tile[32 * q : 32 * q + 32, t0:t1, :], rows[:, t0:t1, :])
+                nc.sync.dma_start(tile[32 * q : 32 * q + 32, t0:t1, :], rows[:, t0:t1, :])
 
         def gather_words(window, idx, name):
             tile = held([P, S], U32, name)
@@ -93,19 +98,6 @@ def tile_list_tinnitus_session_ledger_kernel(
         ident = held([P, P], F32, "ident")
         make_identity(nc, ident[:])
 
-        tab2w = load_words(tab2_words[0], "tab2w")
-        idx2 = load_list(offs2, "idx2")
-        for q in range(QUADS):
-            nc.sync.dma_start(tab2s[32 * q : 32 * q + 4, :].bitcast(I32), tab2_scales[0, 4 * q : 4 * q + 4, :].bitcast(I32))
-        wq_raw = load_words(wq_words[0], "wq_raw")
-        for q in range(QUADS):
-            nc.sync.dma_start(wqs_raw[32 * q : 32 * q + 4, :].bitcast(I32), wq_scales[0, 4 * q : 4 * q + 4, :].bitcast(I32))
-        load_page(0, 0)
-        idx4 = load_list(offs4, "idx4")
-        wg2t = held([P, PACK, S], F32, "wg2t")
-        load_wg(wg2t, wg2, 0, 1)
-        load_page(1, 0)
-
         def load_rows(src, name, tag):
             raw = held([P, PACK, PASS], F32, name, tag)
             nc.sync.dma_start(raw[:], src.rearrange("(p j) c -> p j c", j=PACK))
@@ -115,43 +107,63 @@ def tile_list_tinnitus_session_ledger_kernel(
             return load_rows(wb[a * PASS : (a + 1) * PASS, b * PASS : (b + 1) * PASS], f"wb{a}{b}", tag)
 
         wb_raw = {}
+        wa = [held([P, 2, 2 * PASS], U8, f"wa{b}") for b in range(halves)]
+
+        def load_wa(b):
+            cols = wa_words[:, :, 2 * b * PASS : 2 * (b + 1) * PASS]
+            nc.sync.dma_start(wa[b][:].bitcast(I32), cols.rearrange("a p c -> p a c").bitcast(I32))
+
+        wq_raw = held([P, H], I32, "wq_raw")
+        wq_cols = wq_words[0].rearrange("p c i -> p (c i)").bitcast(I32)
+
+        idx2 = load_list(offs2, "idx2")
+        for q in range(QUADS):
+            nc.sync.dma_start(tab2s[32 * q : 32 * q + 4, :].bitcast(I32), tab2_scales[0, 4 * q : 4 * q + 4, :].bitcast(I32))
+        wg2n = load_wg(wg2, "wg2n")
+        tab2w = load_words(tab2_words[0], "tab2w")
+        nc.sync.dma_start(wq_raw[:, 0:PASS], wq_cols[:, 0:PASS])
+        for q in range(QUADS):
+            nc.sync.dma_start(wqs_raw[32 * q : 32 * q + 4, :].bitcast(I32), wq_scales[0, 4 * q : 4 * q + 4, :].bitcast(I32))
+        load_page(0, 0)
+        idx4 = load_list(offs4, "idx4")
+        load_page(0, 1)
         for q in range(QUADS):
             nc.sync.dma_start(tabs[32 * q : 32 * q + 8, :].bitcast(I32), tab_scales[:, 4 * q : 4 * q + 4, :].bitcast(I32))
         idx = load_list(offs, "idx")
         vs0 = gather_bytes(tabs, idx, "vs0")
         vs = [vs0, vs1]
         tabw = [load_words(tab_words[0], "tabw0")]
-        load_wg(wg2t, wg2, 1, 2)
-        load_page(0, 1)
-        tabw.append(load_words(tab_words[1], "tabw1"))
+        nc.sync.dma_start(wq_raw[:, PASS:H], wq_cols[:, PASS:H])
         for q in range(QUADS):
             nc.sync.dma_start(was[32 * q : 32 * q + 4, :, :].bitcast(I32),
                               wa_scales[:, 4 * q : 4 * q + 4, :].rearrange("a r c -> r a c").bitcast(I32))
-        gain_t = held([P, halves, PACK], F32, "gain_t")
-        nc.sync.dma_start(gain_t[:], gain.rearrange("(b p t) -> p b t", b=halves, t=PACK))
-        load_page(1, 1)
+        load_page(0, 2)
+        tabw.append(load_words(tab_words[1], "tabw1"))
+        load_wa(0)
+        load_page(0, 3)
         for q in range(QUADS):
             nc.sync.dma_start(vs1[32 * q : 32 * q + 4, :].bitcast(I32), vs0[32 * q + 4 : 32 * q + 8, :].bitcast(I32))
-        wa = held([P, 2, 2 * H], U8, "wa")
-        nc.sync.dma_start(wa[:].bitcast(I32), wa_words.rearrange("a p c -> p a c").bitcast(I32))
-        load_wg(wg2t, wg2, 2, 3)
-        load_page(0, 2)
-        load_page(1, 2)
+        gain_t = held([P, halves, PACK], F32, "gain_t")
+        nc.sync.dma_start(gain_t[:], gain.rearrange("(b p t) -> p b t", b=halves, t=PACK))
+        load_page(1, 0)
+        load_page(1, 1)
         wb_raw[0, 0] = load_wb(0, 0, "stage0")
-        load_wg(wg2t, wg2, 3, 4)
-        load_page(0, 3)
+        load_page(1, 2)
         wb_raw[1, 0] = load_wb(1, 0, "stage1")
         load_page(1, 3)
         idx3 = load_list(offs3, "idx3")
         wg1t = held([P, PACK, S], F32, "wg1t")
-        load_wg(wg1t, wg1, 0, 2)
+        load_dealt(wg1t, wg1, 0, 1)
+        load_dealt(wg1t, wg1, 1, 3)
         idx5 = load_list(offs5, "idx5")
         cap_t = held([P, halves, PACK], F32, "cap_t")
         nc.sync.dma_start(cap_t[:], cap.rearrange("(b p t) -> p b t", b=halves, t=PACK))
+        load_wa(1)
         wb_raw[0, 1] = load_wb(0, 1, "stage2")
         wb_raw[1, 1] = load_wb(1, 1, "stage0")
-        load_wg(wg1t, wg1, 2, 4)
+        load_dealt(wg1t, wg1, 3, 4)
         wo_raw = [load_rows(wo[b * PASS : (b + 1) * PASS, :], f"wo{b}", f"stage{b + 1}") for b in range(halves)]
+        wg2t = held([P, PACK, S], F32, "wg2t")
 
         v2w = gather_words(tab2w, idx2, "v2w")
         v2s = gather_bytes(tab2s, idx2, "v2s")
@@ -168,7 +180,7 @@ def tile_list_tinnitus_session_ledger_kernel(
 
         def put_h2(b, t):
             cols = slice(b * PASS + t * P, b * PASS + (t + 1) * P)
-            acc = bank(f"q{b}")
+            acc = bank(f"q{t % 2}")
             mx(acc[:], wq[:, cols], wqs[:, cols], v2w[:], v2s[:], True, True)
             nc.scalar.activation(h2[b][:, t, :], acc[:], ACT.Square)
             nc.vector.tensor_tensor(pages[b, t][:].indirect(idx4[:]), h2[b][:, t, :], wg2t[:, t, :], ALU.mult)
@@ -199,19 +211,32 @@ def tile_list_tinnitus_session_ledger_kernel(
         def blocks(tile):
             return lambda c: tile[:, c * P : (c + 1) * P]
 
+        def turn_weight(natural):
+            turned = bank("w0")
+            turn(turned, blocks(natural))
+            return turned
+
+        def deal_weight(turned, dealt, t, tag):
+            rep = ring2.tile([P, S], F32, name="rep", tag="total_t")
+            rows = turned[:].rearrange("p (c m t) -> p c m t", c=chunks, t=PACK)[:, :, :, t]
+            nc.scalar.copy(rep[:].rearrange("p (c q m) -> p c q m", c=chunks, q=QUADS), rows.unsqueeze(2).to_broadcast([P, chunks, QUADS, 32]))
+            back = bank(tag)
+            turn(back, blocks(rep))
+            nc.scalar.copy(dealt[:, t, :], back[:])
+
         def gained_tanh(b):
             tanh_t = held([P, chunks, PASS], F32, f"tanh_t{b}", ("tanh_t", "stage0")[b])
             for c in range(chunks):
                 tok = slice(c * P, (c + 1) * P)
-                acc = bank(f"a{c % 2}")
+                acc = bank(("a0", "a1", "w0", "w1")[c])
                 for a in range(2):
-                    mx(acc[:], vw[a][:, tok], vs[a][:, tok], wa[:, a, 2 * b * PASS : 2 * (b + 1) * PASS],
+                    mx(acc[:], vw[a][:, tok], vs[a][:, tok], wa[b][:, a, :],
                        was[:, a, b * PASS : (b + 1) * PASS], a == 0, a == 1, FP4X4)
                 nc.scalar.activation(tanh_t[:, c, :].rearrange("p (t m) -> p t m", t=PACK),
                                      acc[:].rearrange("p (m t) -> p t m", t=PACK), ACT.Tanh)
             gained = held([P, PACK, S], F32, f"gained{b}", ("tab2w", "tabw0")[b])
             for t in range(PACK):
-                turned = bank(("x", "y")[t % 2])
+                turned = bank(("x", "y", "q0", "q1")[t])
                 turn(turned, lambda c: tanh_t[:, c, t * P : (t + 1) * P])
                 nc.scalar.activation(gained[:, t, :], turned[:], ACT.Copy, scale=gain_t[:, b, t : t + 1])
             return gained
@@ -270,13 +295,16 @@ def tile_list_tinnitus_session_ledger_kernel(
             nc.vector.quantize_mx(xq[b][:, j0:j1].bitcast(FP8X4), xs[b][:, j0:j1], grouped[:])
 
         wbq = {}
+        wg2_t = turn_weight(wg2n)
+        deal_weight(wg2_t, wg2t, 0, "w1")
         put_h2(0, 0)
-        put_h2(1, 0)
+        for t in range(1, PACK):
+            deal_weight(wg2_t, wg2t, t, f"q{t % 2}")
+            put_h2(0, t)
         vw = [gather_words(tabw[a], idx, f"vw{a}") for a in range(2)]
         for a in range(2):
             wbq[a, 0] = quantise(round_rows(wb_raw[a, 0], True), f"wbq{a}0")
-        for t in range(1, PACK):
-            put_h2(0, t)
+        for t in range(PACK):
             put_h2(1, t)
         gained0 = gained_tanh(0)
         h1a = held([P, PACK, S], F32, "h1a", "h1a")
@@ -297,7 +325,7 @@ def tile_list_tinnitus_session_ledger_kernel(
         for t in range(PACK):
             put_h1(1, t, h1b)
         woq = [quantise(round_rows(wo_raw[b], False), f"woq{b}") for b in range(halves)]
-        g0 = held([P, PACK * PICKS], BF16, "g0", "stage0")
+        g0 = held([P, PACK * PICKS], BF16, "g0", "tabw0")
         for j0 in (0, 512):
             part = g0[:, PACK * j0 : PACK * (j0 + 512)]
             nc.scalar.copy(part.rearrange("p (c i t) -> p c t i", i=4, t=PACK), x0[:, :, j0 : j0 + 512].rearrange("p t (c i) -> p c t i", i=4))

from contextlib import ExitStack

import concourse.mybir as mybir
from concourse.masks import make_identity

F32 = mybir.dt.float32
BF16 = mybir.dt.bfloat16
I32 = mybir.dt.int32
U32 = mybir.dt.uint32
U16 = mybir.dt.uint16
U8 = mybir.dt.uint8
FP8X4 = mybir.dt.float8_e4m3fn_x4
FP4X4 = mybir.dt.float4_e2m1fn_x4
ACT = mybir.ActivationFunctionType
ALU = mybir.AluOpType

K, K2, T, S, H, T2, PICKS, N = 1024, 512, 2048, 512, 1024, 2048, 1024, 512
FLOPS = 2 * K * H * S * 2 + 2 * K2 * H * S + 2 * H * N * PICKS

P = 128
PACK = 4
PASS = P * PACK
QUADS = 4
ALIGN = 64
VEC_ADDS = 2


def tile_list_tinnitus_session_ledger_kernel(
    tc, tab_words, tab_scales, tab2_words, tab2_scales, offs, offs2, offs3, offs4, offs5,
    wa_words, wa_scales, wb, wq_words, wq_scales, gain, page0, wg1, wg2, cap, wo, out,
):
    nc = tc.nc
    halves = H // PASS
    with ExitStack() as ctx:
        keep = ctx.enter_context(tc.tile_pool(name="keep", bufs=1))
        ring2 = ctx.enter_context(tc.tile_pool(name="ring2", bufs=2))
        ring3 = ctx.enter_context(tc.tile_pool(name="ring3", bufs=3))
        psum = ctx.enter_context(tc.psum_pool(name="psum", bufs=1))

        def held(shape, dtype, name, tag=None):
            return keep.tile(shape, dtype, name=name, tag=tag or name, align_bytes=ALIGN)

        def bank(tag):
            return psum.tile([P, PASS], F32, name=tag, tag=tag)

        def load_list(src, name):
            tile = keep.tile(list(src.shape), U16, name=name, tag=name)
            nc.sync.dma_start(tile[:], src)
            return tile

        def zeroed_plane(shape, name):
            tile = held(shape, U8, name)
            nc.vector.memset(tile[:].bitcast(I32), 0)
            return tile

        def load_words(src, name, tag=None):
            cols = src.shape[1]
            tile = held([P, cols], I32, name, tag)
            nc.sync.dma_start(tile[:], src.rearrange("p c i -> p (c i)").bitcast(I32))
            return tile

        page_rows = page0.rearrange("(b p t) c -> b t p c", b=halves, t=PACK)
        pages = {}

        def load_page(b, t):
            pages[b, t] = held([P, T2], F32, f"page{b}{t}")
            nc.sync.dma_start(pages[b, t][:], page_rows[b, t])

        def load_wg(src, name):
            tile = ring2.tile([P, S], F32, name=name, tag="lin")
            nc.sync.dma_start(tile[:], src)
            return tile

        def load_dealt(tile, src, t0, t1):
            rows = src.rearrange("(m t) j -> m t j", t=PACK)
            for q in (0, 2, 1, 3):
                nc.sync.dma_start(tile[32 * q : 32 * q + 32, t0:t1, :], rows[:, t0:t1, :])

        def gather_words(window, idx, name):
            tile = held([P, S], U32, name)
            nc.vector.tensor_copy(tile[:], window[:].bitcast(U32).indirect(idx[:]))
            return tile

        def gather_bytes(window, idx, name):
            tile = held([P, S], U8, name)
            nc.vector.tensor_copy(tile[:], window[:].indirect(idx[:]))
            return tile

        def mx(dst, lhs, lhs_scale, rhs, rhs_scale, start, stop, rhs_fmt=FP8X4):
            nc.tensor.matmul_mx(dst, lhsT=lhs.bitcast(FP8X4), lhsT_scale=lhs_scale,
                                rhs=rhs.bitcast(rhs_fmt), rhs_scale=rhs_scale, start=start, stop=stop)

        tab2s = zeroed_plane([P, T], "tab2s")
        wqs_raw = zeroed_plane([P, H], "wqs_raw")
        tabs = zeroed_plane([P, T], "tabs")
        was = zeroed_plane([P, 2, H], "was")
        vs1 = zeroed_plane([P, S], "vs1")
        ident = held([P, P], F32, "ident")
        make_identity(nc, ident[:])

        def load_rows(src, name, tag):
            raw = held([P, PACK, PASS], F32, name, tag)
            nc.sync.dma_start(raw[:], src.rearrange("(p j) c -> p j c", j=PACK))
            return raw

        def load_wb(a, b, tag):
            return load_rows(wb[a * PASS : (a + 1) * PASS, b * PASS : (b + 1) * PASS], f"wb{a}{b}", tag)

        wb_raw = {}
        wa = [held([P, 2, 2 * PASS], U8, f"wa{b}") for b in range(halves)]

        def load_wa(b):
            cols = wa_words[:, :, 2 * b * PASS : 2 * (b + 1) * PASS]
            nc.sync.dma_start(wa[b][:].bitcast(I32), cols.rearrange("a p c -> p a c").bitcast(I32))

        wq_raw = held([P, H], I32, "wq_raw")
        wq_cols = wq_words[0].rearrange("p c i -> p (c i)").bitcast(I32)

        idx2 = load_list(offs2, "idx2")
        for q in range(QUADS):
            nc.sync.dma_start(tab2s[32 * q : 32 * q + 4, :].bitcast(I32), tab2_scales[0, 4 * q : 4 * q + 4, :].bitcast(I32))
        wg2n = load_wg(wg2, "wg2n")
        tab2w = load_words(tab2_words[0], "tab2w")
        nc.sync.dma_start(wq_raw[:, 0:PASS], wq_cols[:, 0:PASS])
        for q in range(QUADS):
            nc.sync.dma_start(wqs_raw[32 * q : 32 * q + 4, :].bitcast(I32), wq_scales[0, 4 * q : 4 * q + 4, :].bitcast(I32))
        load_page(0, 0)
        idx4 = load_list(offs4, "idx4")
        load_page(0, 1)
        for q in range(QUADS):
            nc.sync.dma_start(tabs[32 * q : 32 * q + 8, :].bitcast(I32), tab_scales[:, 4 * q : 4 * q + 4, :].bitcast(I32))
        idx = load_list(offs, "idx")
        vs0 = gather_bytes(tabs, idx, "vs0")
        vs = [vs0, vs1]
        tabw = [load_words(tab_words[0], "tabw0")]
        nc.sync.dma_start(wq_raw[:, PASS:H], wq_cols[:, PASS:H])
        for q in range(QUADS):
            nc.sync.dma_start(was[32 * q : 32 * q + 4, :, :].bitcast(I32),
                              wa_scales[:, 4 * q : 4 * q + 4, :].rearrange("a r c -> r a c").bitcast(I32))
        load_page(0, 2)
        tabw.append(load_words(tab_words[1], "tabw1"))
        load_wa(0)
        load_page(0, 3)
        for q in range(QUADS):
            nc.sync.dma_start(vs1[32 * q : 32 * q + 4, :].bitcast(I32), vs0[32 * q + 4 : 32 * q + 8, :].bitcast(I32))
        gain_t = held([P, halves, PACK], F32, "gain_t")
        nc.sync.dma_start(gain_t[:], gain.rearrange("(b p t) -> p b t", b=halves, t=PACK))
        load_page(1, 0)
        load_page(1, 1)
        wb_raw[0, 0] = load_wb(0, 0, "stage0")
        load_page(1, 2)
        wb_raw[1, 0] = load_wb(1, 0, "stage1")
        load_page(1, 3)
        idx3 = load_list(offs3, "idx3")
        wg1t = held([P, PACK, S], F32, "wg1t")
        load_dealt(wg1t, wg1, 0, 1)
        load_dealt(wg1t, wg1, 1, 3)
        idx5 = load_list(offs5, "idx5")
        cap_t = held([P, halves, PACK], F32, "cap_t")
        nc.sync.dma_start(cap_t[:], cap.rearrange("(b p t) -> p b t", b=halves, t=PACK))
        load_wa(1)
        wb_raw[0, 1] = load_wb(0, 1, "stage2")
        wb_raw[1, 1] = load_wb(1, 1, "stage0")
        load_dealt(wg1t, wg1, 3, 4)
        wo_raw = [load_rows(wo[b * PASS : (b + 1) * PASS, :], f"wo{b}", f"stage{b + 1}") for b in range(halves)]
        wg2t = held([P, PACK, S], F32, "wg2t")

        v2w = gather_words(tab2w, idx2, "v2w")
        v2s = gather_bytes(tab2s, idx2, "v2s")
        wqs = held([P, H], U8, "wqs")
        wq = held([P, H], I32, "wq")
        for b in range(halves):
            cols = slice(b * PASS, (b + 1) * PASS)
            nc.vector.tensor_copy(wq[:, cols].rearrange("p (t c i) -> p c t i", t=PACK, i=4),
                                  wq_raw[:, cols].rearrange("p (c i t) -> p c t i", t=PACK, i=4))
            nc.vector.tensor_copy(wqs[:, cols].rearrange("p (t c i) -> p c t i", t=PACK, i=16),
                                  wqs_raw[:, cols].rearrange("p (c i t) -> p c t i", t=PACK, i=16))

        h2 = [held([P, PACK, S], F32, f"h2_{b}", f"half{b}") for b in range(halves)]

        def put_h2(b, t):
            cols = slice(b * PASS + t * P, b * PASS + (t + 1) * P)
            acc = bank(f"q{t % 2}")
            mx(acc[:], wq[:, cols], wqs[:, cols], v2w[:], v2s[:], True, True)
            nc.scalar.activation(h2[b][:, t, :], acc[:], ACT.Square)
            nc.vector.tensor_tensor(pages[b, t][:].indirect(idx4[:]), h2[b][:, t, :], wg2t[:, t, :], ALU.mult)

        def round_rows(raw, deal):
            grouped = ring3.tile([P, PACK * PASS], BF16, name="grouped", tag="grouped", align_bytes=ALIGN)
            if deal:
                nc.scalar.copy(grouped[:].rearrange("p (t m j) -> p m j t", t=PACK, j=PACK),
                               raw[:].rearrange("p j (m t) -> p m j t", t=PACK))
            else:
                nc.scalar.copy(grouped[:].rearrange("p (c i j) -> p c j i", i=4, j=PACK),
                               raw[:].rearrange("p j (c i) -> p c j i", i=4))
            return grouped

        def quantise(grouped, name):
            codes = held([P, PASS], U32, name)
            scales = held([P, PASS], U8, name + "s")
            nc.vector.quantize_mx(codes[:].bitcast(FP8X4), scales[:], grouped[:])
            return codes, scales

        chunks = S // P

        def turn(dst, src, start=True, stop=True):
            for c in range(chunks):
                cols = slice(c * P, (c + 1) * P)
                nc.tensor.matmul(dst[:, cols], src(c), ident[:], start=start and c == 0, stop=stop and c == chunks - 1, is_transpose=True)

        def blocks(tile):
            return lambda c: tile[:, c * P : (c + 1) * P]

        def turn_weight(natural):
            turned = bank("w0")
            turn(turned, blocks(natural))
            return turned

        def deal_weight(turned, dealt, t, tag):
            rep = ring2.tile([P, S], F32, name="rep", tag="total_t")
            rows = turned[:].rearrange("p (c m t) -> p c m t", c=chunks, t=PACK)[:, :, :, t]
            nc.scalar.copy(rep[:].rearrange("p (c q m) -> p c q m", c=chunks, q=QUADS), rows.unsqueeze(2).to_broadcast([P, chunks, QUADS, 32]))
            back = bank(tag)
            turn(back, blocks(rep))
            nc.scalar.copy(dealt[:, t, :], back[:])

        def gained_tanh(b):
            tanh_t = held([P, chunks, PASS], F32, f"tanh_t{b}", ("tanh_t", "stage0")[b])
            for c in range(chunks):
                tok = slice(c * P, (c + 1) * P)
                acc = bank(("a0", "a1", "w0", "w1")[c])
                for a in range(2):
                    mx(acc[:], vw[a][:, tok], vs[a][:, tok], wa[b][:, a, :],
                       was[:, a, b * PASS : (b + 1) * PASS], a == 0, a == 1, FP4X4)
                nc.scalar.activation(tanh_t[:, c, :].rearrange("p (t m) -> p t m", t=PACK),
                                     acc[:].rearrange("p (m t) -> p t m", t=PACK), ACT.Tanh)
            gained = held([P, PACK, S], F32, f"gained{b}", ("tab2w", "tabw0")[b])
            for t in range(PACK):
                turned = bank(("x", "y", "q0", "q1")[t])
                turn(turned, lambda c: tanh_t[:, c, t * P : (t + 1) * P])
                nc.scalar.activation(gained[:, t, :], turned[:], ACT.Copy, scale=gain_t[:, b, t : t + 1])
            return gained

        def linear(b, t, tag):
            acc = bank(tag)
            for a in range(2):
                codes, scales = wbq[a, b]
                mx(acc[:], codes[:, t * P : (t + 1) * P], scales[:, t * P : (t + 1) * P], vw[a][:], vs[a][:], a == 0, a == 1)
            return acc

        def add_on_vector(b, t, gained, h1):
            nc.vector.tensor_tensor(h1[:, t, :], linear(b, t, ("q0", "q1", "w0", "w1")[t])[:], gained[:, t, :], ALU.add)

        def add_on_tensor(b, t, gained, h1):
            lin = ring2.tile([P, S], F32, name="lin", tag="lin")
            nc.scalar.copy(lin[:], linear(b, t, f"{'aq'[b]}{t % 2}")[:])
            total = bank(f"w{t % 2}")
            turn(total, blocks(gained[:, t, :]), stop=False)
            turn(total, blocks(lin), start=False)
            total_t = ring2.tile([P, S], F32, name="total_t", tag="total_t")
            nc.scalar.copy(total_t[:], total[:])
            back = bank(("x", "y")[t % 2])
            turn(back, blocks(total_t))
            nc.scalar.copy(h1[:, t, :], back[:])

        def put_h1(b, t, h1):
            nc.vector.tensor_tensor(pages[b, t][:].indirect(idx3[:]), h1[:, t, :], wg1t[:, t, :], ALU.mult)

        xq = [held([P, PICKS], U32, "xq0", "wq_raw"), held([P, PICKS], U32, "xq1", "wq")]
        xs = [held([P, PICKS], U8, f"xs{b}") for b in range(halves)]

        def fetch(b, j0, j1, tag):
            xf = held([P, PACK, j1 - j0], F32, f"xf{b}_{j0}", tag)

            def cap_at(t):
                nc.vector.tensor_scalar(xf[:, t, :], xf[:, t, :], cap_t[:, b, t : t + 1], None, ALU.min)

            for t in range(PACK):
                nc.vector.tensor_copy(xf[:, t, :], pages[b, t][:].indirect(idx5[:, j0 // 16 : j1 // 16]))
                if t > 0:
                    cap_at(t - 1)
            cap_at(PACK - 1)
            return xf

        def weave(xf, copy, tag=None):
            width = xf.shape[2]
            if tag:
                grouped = held([P, PACK * width], BF16, "xgrouped", tag)
            else:
                grouped = ring3.tile([P, PACK * width], BF16, name="xgrouped", tag="grouped", align_bytes=ALIGN)
            copy(grouped[:].rearrange("p (c i t) -> p c t i", i=4, t=PACK), xf.rearrange("p t (c i) -> p c t i", i=4))
            return grouped

        def quantise_x(b, j0, j1, grouped):
            nc.vector.quantize_mx(xq[b][:, j0:j1].bitcast(FP8X4), xs[b][:, j0:j1], grouped[:])

        wbq = {}
        wg2_t = turn_weight(wg2n)
        deal_weight(wg2_t, wg2t, 0, "w1")
        put_h2(0, 0)
        for t in range(1, PACK):
            deal_weight(wg2_t, wg2t, t, f"q{t % 2}")
            put_h2(0, t)
        vw = [gather_words(tabw[a], idx, f"vw{a}") for a in range(2)]
        for a in range(2):
            wbq[a, 0] = quantise(round_rows(wb_raw[a, 0], True), f"wbq{a}0")
        for t in range(PACK):
            put_h2(1, t)
        gained0 = gained_tanh(0)
        h1a = held([P, PACK, S], F32, "h1a", "h1a")
        for t in range(PACK):
            if t < VEC_ADDS:
                add_on_vector(0, t, gained0, h1a)
            else:
                add_on_tensor(0, t, gained0, h1a)
        for t in range(PACK):
            put_h1(0, t, h1a)
        for a in range(2):
            wbq[a, 1] = quantise(round_rows(wb_raw[a, 1], True), f"wbq{a}1")
        gained1 = gained_tanh(1)
        x0 = fetch(0, 0, PICKS, "h1a")
        h1b = held([P, PACK, S], F32, "h1b", "half1")
        for t in range(PACK):
            add_on_tensor(1, t, gained1, h1b)
        for t in range(PACK):
            put_h1(1, t, h1b)
        woq = [quantise(round_rows(wo_raw[b], False), f"woq{b}") for b in range(halves)]
        g0 = held([P, PACK * PICKS], BF16, "g0", "tabw0")
        for j0 in (0, 512):
            part = g0[:, PACK * j0 : PACK * (j0 + 512)]
            nc.scalar.copy(part.rearrange("p (c i t) -> p c t i", i=4, t=PACK), x0[:, :, j0 : j0 + 512].rearrange("p t (c i) -> p c t i", i=4))
            nc.vector.quantize_mx(xq[0][:, j0 : j0 + 512].bitcast(FP8X4), xs[0][:, j0 : j0 + 512], part)

        out_rows = out.rearrange("(n p) j -> p n j", p=P)

        def project_pass(dst, nt, b, j0, j1, start, stop):
            codes, scales = woq[b]
            cols = slice(nt * P, (nt + 1) * P)
            mx(dst, codes[:, cols], scales[:, cols], xq[b][:, j0:j1], xs[b][:, j0:j1], start, stop)

        def project_narrow(banks, b, j0):
            for nt in range(4):
                e = nt % 2
                project_pass(banks[nt // 2][:, e * 256 : (e + 1) * 256], nt, b, j0, j0 + 256, b == 0 and e == 0, b == 1 and e == 1)

        first = [bank(tag) for tag in ("q0", "q1", "a0", "a1")]
        second = [bank(tag) for tag in ("w0", "w1")]
        third = [bank(tag) for tag in ("x", "y")]
        for nt in range(4):
            project_pass(first[nt][:], nt, 0, 0, 512, True, False)
        project_narrow(second, 0, 512)
        project_narrow(third, 0, 768)
        x2 = fetch(1, 0, 512, "half1")
        g2 = weave(x2[:], nc.scalar.copy, "wg2t")
        x3 = fetch(1, 512, 768, "wg1t")
        quantise_x(1, 0, 512, g2)
        g3 = weave(x3[:], nc.scalar.copy)
        quantise_x(1, 512, 768, g3)
        x4 = fetch(1, 768, 1024, "wg2t")

        staged = held([P, PACK, 512], F32, "staged0", "stage1")
        for nt in range(4):
            project_pass(first[nt][:], nt, 1, 0, 512, False, True)
            nc.scalar.copy(staged[:, nt, :], first[nt][:])
            if nt % 2 == 1:
                nc.sync.dma_start(out_rows[:, nt - 1 : nt + 1, 0:512], staged[:, nt - 1 : nt + 1, :])

        staged = held([P, PACK, 256], F32, "staged1", "stage2")
        project_narrow(second, 1, 512)
        for pair in range(2):
            nc.scalar.copy(staged[:, 2 * pair : 2 * pair + 2, :], second[pair][:].rearrange("p (e j) -> p e j", e=2))
        nc.sync.dma_start(out_rows[:, :, 512:768], staged[:])

        quantise_x(1, 768, 1024, weave(x4[:], nc.vector.tensor_copy))
        staged = held([P, PACK, 256], F32, "staged2", "tanh_t")
        project_narrow(third, 1, 768)
        for pair, (copy, queue) in enumerate(((nc.vector.tensor_copy, nc.sync), (nc.scalar.copy, nc.scalar))):
            copy(staged[:, 2 * pair : 2 * pair + 2, :], third[pair][:].rearrange("p (e j) -> p e j", e=2))
            queue.dma_start(out_rows[:, 2 * pair : 2 * pair + 2, 768:1024], staged[:, 2 * pair : 2 * pair + 2, :])
